import numpy as np, ml_dtypes
CORES = [51,54,179,182]
N = 4
BF = ml_dtypes.bfloat16
def gentries(a):
    return np.ascontiguousarray(a.reshape(8, 16, -1).transpose(0, 2, 1)).reshape(8, -1)
def gtable(e):
    e = np.asarray(e); return np.ascontiguousarray(e.reshape(8, -1, 16).transpose(0, 2, 1)).reshape(128, -1).astype(np.int32)
H, E, L = 2048, 64, 2
M = (N - 1) * E
def slot(r, q):
    return q - (1 if q > r else 0)
def flat(a):
    return np.ascontiguousarray(np.asarray(a).astype(np.int64).transpose(1, 0, 2)).reshape(8, -1)
def perms(rng):
    return np.argsort(rng.random((N, 8, H)), axis=-1)
def mesh(c, w, lens):
    nx, pv, tw = np.empty((N, 8, H), np.int64), np.empty((N, 8, H), np.int64), np.empty((N, 8, H), np.int64)
    for r in range(N):
        for g in range(8):
            e = np.add.accumulate(lens[r, g]); e = np.append(e[e < H], H); s = np.append(0, e[:-1])
            k = np.arange(1, H + 1); k[e - 1] = s; a = w[r, g]
            nx[r, g, a] = H * r + a[k]; pv[r, g, a[k]] = H * r + a
            b = c[r, g, M:].reshape(-1, 2); tw[r, g, b] = H * r + b[:, ::-1]
            for q in range(N):
                if q != r:
                    i, j = E * slot(r, q), E * slot(q, r)
                    tw[r, g, c[r, g, i:i + E]] = H * q + c[q, g, j:j + E]
    return {"nxt": nx.astype(np.int32), "prv": pv.astype(np.int32), "twn": tw.astype(np.int32), "far": np.stack([gtable(c[r, :, :M]) for r in range(N)])}
def draw(v, c, w, lens):
    d = {"x": v.astype(np.float32).astype(BF)}; d.update(mesh(c, w, lens)); return d
def setup_inputs(rng):
    v = rng.integers(-31, 32, (N, 128, H))
    return draw(v, perms(rng), perms(rng), rng.integers(3, 9, (N, 8, H)))
def setup_inputs_long(rng):
    v = rng.integers(-31, 32, (N, 128, H)); k = (np.arange(N)[:, None] + np.arange(8) + rng.integers(0, 3)) % 3
    lens = rng.integers(1, 3, (N, 8, H)); lens[k == 0] = H
    lens = np.where((k == 2)[:, :, None], rng.integers(1, 201, (N, 8, H)), lens)
    return draw(v, perms(rng), perms(rng), lens)
def setup_inputs_near(rng):
    v = np.where(rng.random((N, 128, H)) < 0.875, 31, -31); a = np.arange(H)
    e = np.append(a[:M // 2], a[H - M // 2:]); mid = a[M // 2:H - M // 2]; c = np.empty((N, 8, H), np.int64); c[:, :, M:] = mid
    for r in range(N):
        for g in range(8): c[r, g, :M] = rng.permutation(e)
    w = np.broadcast_to(a, (N, 8, H))
    return draw(v, c, w, rng.integers(2, 6, (N, 8, H)))
def setup_inputs_hops(rng):
    v = rng.integers(-31, 32, (N, 128, H)); c = perms(rng); w = c.copy()
    for r in range(N):
        for g in range(4): w[r, g, :M] = rng.permutation(c[r, g, :M])
    return draw(v, c, w, rng.integers(3, 17, (N, 8, H)))
def setup_inputs_spread(rng):
    v = (rng.integers(-31, 32, (N, 128, H)) >> rng.integers(0, 5, (N, 1, H))) * (rng.random((N, 1, H)) > 0.0625)
    return draw(v, perms(rng), perms(rng), 2 ** rng.integers(0, 8, (N, 8, H)))
def check_inputs(d):
    bad = []
    try:
        v = np.asarray(d["x"]).astype(np.float32)
        if not (v.shape == (N, 128, H) and np.isfinite(v).all() and (np.abs(v) <= 31).all() and (v == np.floor(v)).all()): bad.append("x: whole numbers from -31 to 31")
        nx, pv, tw = [np.asarray(d[k]).astype(np.int64) for k in ("nxt", "prv", "twn")]
        own = np.broadcast_to(np.arange(N)[:, None, None], (N, 8, H))
        if not all(a.shape == (N, 8, H) and (a >= 0).all() and (a < N * H).all() for a in (nx, pv, tw)): return bad + ["nxt, prv, twn: range"]
        if not ((nx // H == own).all() and (pv // H == own).all()): bad.append("nxt, prv: same rank")
        n, p, t = flat(nx), flat(pv), flat(tw); me = np.arange(N * H)
        if any((p[g][n[g]] != me).any() or (n[g][p[g]] != me).any() for g in range(8)): bad.append("nxt and prv: one undoes the other")
        if any((t[g][t[g]] != me).any() or (t[g] == me).any() for g in range(8)): bad.append("twn: pairs")
        for r in range(N):
            for q in range(N):
                if q != r and (np.sum(tw[r] // H == q, axis=1) != E).any(): bad.append("twn: E far twins a pair")
        f = np.stack([gentries(np.asarray(a).astype(np.int64)) for a in d["far"]])
        if not (f.shape == (N, 8, M) and (f >= 0).all() and (f < H).all()): return bad + ["far: range"]
        u = np.sort(f, axis=-1)
        if (u[..., 1:] == u[..., :-1]).any(): bad.append("far: all different")
        for r in range(N):
            for q in range(N):
                if q != r:
                    i, j = E * slot(r, q), E * slot(q, r)
                    if any((tw[r, g][f[r, g, i:i + E]] != H * q + f[q, g, j:j + E]).any() for g in range(8)): bad.append("far: order")
    except Exception:
        bad.append("shapes")
    return bad
def reference(x, nxt, prv, twn, far):
    v = x.astype(np.float32).reshape(N, 8, 16, H).transpose(1, 2, 0, 3).reshape(8, 16, N * H)
    n, p, t = flat(nxt), flat(prv), flat(twn)
    for k in range(L):
        W = v.shape[2]; v2 = np.empty((8, 16, 2 * W), np.float32); n2, p2 = np.empty((8, 2 * W), np.int64), np.empty((8, 2 * W), np.int64)
        for g in range(8):
            m = v[g] + v[g][:, n[g]]
            v2[g, :, 0::2] = m; v2[g, :, 1::2] = m[:, n[g]]
            n2[g, 0::2] = 2 * n[g]; n2[g, 1::2] = 2 * p[g][t[g]] + 1
            p2[g, 0::2] = 2 * p[g]; p2[g, 1::2] = 2 * t[g][n[g]] + 1
        v, n, p = v2, n2, p2; t = np.broadcast_to(np.arange(2 * W) ^ 1, (8, 2 * W))
    y = v.reshape(8, 16, N, -1)[..., 1::2].transpose(2, 0, 1, 3)
    return {"y": np.ascontiguousarray(y).reshape(N, 128, -1).astype(BF), "nx": np.ascontiguousarray(n.reshape(8, N, -1).transpose(1, 0, 2)).astype(np.float32)}

@@ -1,0 +1,312 @@
+from concourse.bass import DstId, RemoteDMATransfer
+from concourse.mybir import AluOpType, ActivationFunctionType
+
+H = 2048
+NR = 4
+E = 64
+M3 = 192
+BLK = 408
+O_CODE, O_SB, O_EB, O_EC = 64, 88, 280, 344
+O_E = (0, O_EB, O_EC)
+SENT = ((0, O_EB), (O_CODE, O_EC), (O_CODE, BLK))
+UV = 512
+CH = (0, 512, 1024, 1536, 1792, 2048)
+
+SCRATCH = {
+    "X": ("sbuf", [128, H], "bfloat16"),
+    "X2": ("sbuf", [128, H], "bfloat16"),
+    "M2": ("sbuf", [128, H], "bfloat16"),
+    "U2": ("sbuf", [128, H], "bfloat16"),
+    "Mb": ("sbuf", [128, H], "bfloat16"),
+    "Zb": ("sbuf", [128, H], "bfloat16"),
+    "UE": ("sbuf", [128, H + M3], "bfloat16"),
+    "Y": ("sbuf", [128, 2 * H], "bfloat16"),
+    "W": ("sbuf", [128, H], "bfloat16"),
+    "WZ": ("sbuf", [128, H], "bfloat16"),
+    "GP": ("sbuf", [128, H], "bfloat16"),
+    "GT": ("sbuf", [128, H], "bfloat16"),
+    "ZN": ("sbuf", [128, NR * BLK], "bfloat16"),
+    "G0": ("sbuf", [128, M3], "bfloat16"),
+    "G1": ("sbuf", [128, 2 * M3], "bfloat16"),
+    "PL": ("sbuf", [128, M3], "bfloat16"),
+    "ZT": ("sbuf", [128, M3], "bfloat16"),
+    "IOT": ("sbuf", [128, M3], "bfloat16"),
+    "SEL": ("sbuf", [128, 288], "bfloat16"),
+    "ONES": ("sbuf", [128, 8], "bfloat16"),
+    "T8": ("sbuf", [128, 16], "bfloat16"),
+    "AT": ("sbuf", [128, 256], "int32"),
+    "AN": ("sbuf", [128, 128], "int32"),
+    "IN": ("sbuf", [128, 4, 64], "int32"),
+    "FAR": ("sbuf", [128, 12], "int32"),
+    "HI": ("sbuf", [128, 256], "bfloat16"),
+    "LO": ("sbuf", [128, 256], "bfloat16"),
+    "F": ("sbuf", [128, 256], "float32"),
+    "FT": ("sbuf", [128, 256], "float32"),
+    "L": ("sbuf", [128, 256], "uint16"),
+    "LS": ("sbuf", [128, 24], "uint16"),
+    "PF": ("sbuf", [128, 12], "uint16"),
+    "CL16": ("sbuf", [128, 12], "uint16"),
+    "PT16": ("sbuf", [128, 128], "uint16"),
+    "PTa": ("sbuf", [128, 128], "float32"),
+    "PTb": ("sbuf", [128, 128], "float32"),
+    "KI": ("sbuf", [128, 4], "int32"),
+    "KF": ("sbuf", [128, 8], "float32"),
+    "IC": ("sbuf", [128, 12], "float32"),
+    "EL": ("sbuf", [128, 12], "float32"),
+    "C1": ("sbuf", [128, 12], "float32"),
+    "C2": ("sbuf", [128, 12], "float32"),
+    "C3": ("sbuf", [128, 12], "float32"),
+    "CL": ("sbuf", [128, 12], "float32"),
+    "NX": ("sbuf", [128, 512], "float32"),
+    "P0": ("psum", [128, 512], "float32"),
+    "P1": ("psum", [128, 512], "float32"),
+    "P2": ("psum", [128, 512], "float32"),
+    "P3": ("psum", [128, 512], "float32"),
+    "P4": ("psum", [128, 512], "float32"),
+    "P5": ("psum", [128, 512], "float32"),
+}
+SEMAPHORES = ["sv", "ss", "sp", "sg", "ldA", "ldF", "ldI", "ldX", "ldN", "ldW", "st", "a0", "a1c", "a1o", "l0", "l1",
+              "x2a", "x2b", "x2c", "m2a", "m2b", "u2"]
+
+
+def peers(T, topo, r):
+    c = T.cores[r]
+    near = [q for q in range(NR) if q != r and T.cores[q] in topo.cores_of(c)]
+    away = [q for q in range(NR) if q != r and q not in near]
+    return away + near
+
+
+def bits(es):
+    m = 0
+    for e in es:
+        m |= 1 << e
+    return m
+
+
+def rank_program(g, core, T, topo):
+    r = T.rank_of(core)
+    if r is None:
+        return
+    A = AluOpType
+    ID = ActivationFunctionType.Identity
+    CP = ActivationFunctionType.Copy
+    Q = {"v": g.vector, "s": g.scalar, "p": g.tensor, "g": g, "y": g.sync}
+    own = {"v": "sv", "s": "ss", "p": "sp", "g": "sg"}
+    count = {"v": 0, "s": 0, "p": 0, "g": 0}
+    seen = {k: {} for k in Q}
+
+    def wait(q, deps):
+        need = {}
+        for s, n in deps:
+            need[s] = max(need.get(s, 0), n)
+        for s, n in need.items():
+            if seen[q].get(s, 0) < n:
+                Q[q].wait_ge(T.sem[s], n)
+                seen[q][s] = n
+
+    def op(q, deps, make):
+        wait(q, deps)
+        make().then_inc(T.sem[own[q]], 1)
+        count[q] += 1
+        return (own[q], count[q])
+
+    def copy(out, in_, sem, deps):
+        wait("y", deps)
+        g.sync.dma_start(out, in_).then_inc(T.sem[sem], 16)
+
+    V, S, P = g.vector, g.scalar, g.tensor
+    base = float(H * r)
+    pr = peers(T, topo, r)
+    kind = [peers(T, topo, q).index(r) for q in pr]
+    slot = [q - (1 if q > r else 0) for q in pr]
+    blk = BLK * r
+
+    g.sync.dma_start(T.AT[:, 0:128], T.twn[:]).then_inc(T.sem.ldA, 16)
+    S.dma_start(T.AT[:, 128:256], T.prv[:]).then_inc(T.sem.ldA, 16)
+    g.sync.dma_start(T.FAR[:], T.far[:]).then_inc(T.sem.ldF, 16)
+    S.dma_start(T.IN[:, 0, :], T.nxt[0::2, :]).then_inc(T.sem.ldI, 16)
+    g.sync.dma_start(T.IN[:, 1, :], T.nxt[1::2, :]).then_inc(T.sem.ldI, 16)
+    S.dma_start(T.IN[:, 2, :], T.twn[0::2, :]).then_inc(T.sem.ldI, 16)
+    g.sync.dma_start(T.IN[:, 3, :], T.twn[1::2, :]).then_inc(T.sem.ldI, 16)
+    S.dma_start(T.X[:], T.x[:]).then_inc(T.sem.ldX, 16)
+    g.sync.dma_start(T.X2[:, 0:512], T.x[:, 0:512]).then_inc(T.sem.x2a, 16)
+    ldA, ldF, ldI, ldX, ldN, ldW = ("ldA", 32), ("ldF", 16), ("ldI", 64), ("ldX", 16), ("ldN", 16), ("ldW", 64)
+
+    ki = op("g", [], lambda: g.iota(T.KI[:, 0:1], [[0, 1]], 0, 1))
+    wz0 = op("v", [], lambda: V.memset(T.WZ[:, 0:512], 0.0))
+    sel0 = op("v", [], lambda: V.memset(T.SEL[:], 0.0))
+    ones = op("v", [], lambda: V.memset(T.ONES[:], 1.0))
+    r3 = op("v", [ki], lambda: V.tensor_scalar(T.KI[:, 1:2], T.KI[:, 0:1], 3, None, A.bitwise_and))
+    r1 = op("v", [ki], lambda: V.tensor_scalar(T.KI[:, 2:3], T.KI[:, 0:1], 1, None, A.bitwise_and))
+    r15 = op("v", [ki], lambda: V.tensor_scalar(T.KI[:, 3:4], T.KI[:, 0:1], 15, None, A.bitwise_and))
+    w0 = op("v", [], lambda: V.memset(T.W[:], 0.0))
+    op("v", [r15], lambda: V.tensor_copy(T.KF[:, 0:2], T.KI[:, 2:4]))
+    op("v", [r3], lambda: V.tensor_scalar(T.KF[:, 2:3], T.KI[:, 1:2], 2.0, float(H), A.is_equal, A.mult))
+    kf = op("v", [r3], lambda: V.tensor_scalar(T.KF[:, 3:4], T.KI[:, 1:2], 0.0, None, A.is_equal))
+
+    iot = op("g", [], lambda: g.iota(T.IOT[:], [[1, M3]], 0, 0, allow_small_or_imprecise_dtypes=True))
+    t8a = op("g", [ones], lambda: g.affine_select(T.T8[:, 0:8], T.ONES[:], [[-16, 8]], A.is_ge, 0.0, 0, 1))
+    t8b = op("g", [ones], lambda: g.affine_select(T.T8[:, 8:16], T.ONES[:], [[-16, 8]], A.is_ge, 0.0, -2, 1))
+    op("g", [t8a, sel0], lambda: g.affine_select(T.SEL[:, 16:144:16], T.T8[:, 0:8], [[16, 8]], A.is_ge, 0.0, 1, -1))
+    sel = op("g", [t8b, sel0], lambda: g.affine_select(T.SEL[:, 160:288:16], T.T8[:, 8:16], [[16, 8]], A.is_ge, 0.0, 3, -1))
+    for k in range(3):
+        ic = op("g", [], lambda: g.iota(T.IC[:, 4 * k:4 * k + 4], [[16, 4]], blk + O_E[k], 0,
+                                        allow_small_or_imprecise_dtypes=True))
+
+    for k in range(1, 4):
+        wz = op("s", [wz0], lambda: S.activation(T.WZ[:, 512 * k:512 * k + 512], T.WZ[:, 0:512], CP))
+    gaps = []
+    for k in range(3):
+        lo_, hi_ = SENT[kind[k]]
+        for a, b in ((0, lo_), (hi_, BLK)):
+            if b > a:
+                gaps.append(op("s", [wz0], lambda: S.activation(T.ZN[:, BLK * pr[k] + a:BLK * pr[k] + b], T.WZ[:, 0:b - a], CP)))
+    bcol = []
+    for k in range(3):
+        ck = float(BLK * pr[k] + O_SB + E * kind[k] - E * k)
+        bcol.append(op("s", [kf], lambda: S.activation(T.KF[:, 4 + k:5 + k], T.KF[:, 3:4], ID, bias=T.KF[:, 2:3], scale=ck)))
+    for k in range(3):
+        zt = op("s", [bcol[k], iot, kf], lambda: S.activation(T.ZT[:, E * k:E * k + E], T.IOT[:, E * k:E * k + E], ID,
+                                                              bias=T.KF[:, 4 + k:5 + k], scale=T.KF[:, 0:1]))
+
+    hi = op("v", [ldA], lambda: V.tensor_copy(T.HI[:], T.AT[:]))
+    for k in range(3):
+        fl = op("v", [ldF], lambda: V.tensor_copy(T.LS[:, 4 + 4 * k:8 + 4 * k], T.FAR[:, 4 * slot[k]:4 * slot[k] + 4]))
+    lo = op("v", [hi], lambda: V.tensor_tensor(T.LO[:], T.AT[:], T.HI[:], A.subtract))
+    copy(T.W[0::16, :], T.HI[:, 0:128], "ldW", [hi, w0])
+    copy(T.W[2::16, :], T.HI[:, 128:256], "ldW", [])
+    copy(T.W[1::16, :], T.LO[:, 0:128], "ldW", [lo])
+    wait("s", [lo, w0])
+    S.dma_start(T.W[3::16, :], T.LO[:, 128:256]).then_inc(T.sem.ldW, 16)
+    copy(T.X2[:, 512:1024], T.x[:, 512:1024], "x2b", [])
+    copy(T.X2[:, 1024:H], T.x[:, 1024:H], "x2c", [])
+    copy(T.AN[:], T.nxt[:], "ldN", [])
+    el = op("s", [ic, kf], lambda: S.activation(T.EL[:], T.IC[:], ID, bias=T.KF[:, 1:2]))
+
+    for b in range(4):
+        f = op("v", [ldI], lambda: V.tensor_scalar(T.F[:, 64 * b:64 * b + 64], T.IN[:, :, 16 * b:16 * b + 16], base, None, A.subtract))
+    ft = op("v", [f], lambda: V.transpose(T.FT[:], T.F[:]))
+    for b in range(4):
+        lst = op("v", [ft], lambda: V.tensor_scalar(T.L[:, b::4], T.FT[:, 64 * b:64 * b + 64], float(H - 1), None, A.min))
+    far = T.LS[:, 4:16]
+    zs = op("v", [fl, zt, wz, wz0] + gaps, lambda: V.tensor_copy(T.WZ[:].indirect(far), T.ZT[:]))
+
+    def nl(a, b):
+        return T.L[:, a // 16:b // 16]
+
+    def tl(a, b):
+        return T.L[:, 128 + a // 16:128 + b // 16]
+
+    def extract(out, s, src, n, stepped, deps, half=()):
+        wait("p", deps + [sel])
+        for a in range(16):
+            if a == 8:
+                wait("p", half)
+            rhs = src[:, a:16 * n:16] if stepped else src[:, n * a:n * a + n]
+            ins = P.matmul(out[:, 0:n], T.SEL[:, 144 * s + 16 - a:144 * s + 144 - a], rhs, a == 0, a == 15)
+        ins.then_inc(T.sem.sp, 1)
+        count["p"] += 1
+        return ("sp", count["p"])
+
+    def pick(out, win, off, deps):
+        return op("s", deps, lambda: S.activation(out, win.indirect(off), CP))
+
+    def pick_add(out, win, off, in1, deps):
+        return op("v", deps, lambda: V.tensor_tensor(out, win.indirect(off), in1, A.add))
+
+    def send(parts, lsem):
+        tr = []
+        for q, es, src, dst, sem in parts:
+            rid, pid = topo.addr(T.cores[q], core)
+            tr.append(RemoteDMATransfer(dst_ids=[DstId(rid=rid, pnc=pid)], dma_engine_mask=bits(es), remote_sem=sem, src=src, dst=dst))
+        g.remote_dma_fused(tr, local_sem=lsem)
+
+    off = topo.engines(core, T.cores[pr[0]])
+    on = [e for e in topo.engines(core, T.cores[pr[2]]) if e not in off]
+    eng = [off[:len(off) // 2], off[len(off) // 2:], on]
+    n_off, n_on = len(off), len(on)
+
+    g0 = pick(T.G0[:], T.W[:], far, [ldW, fl])
+    wait("g", [g0])
+    send([(pr[k], eng[k], T.G0[:, E * k:E * k + E], T.PL[:, E * kind[k]:E * kind[k] + E], T.sem.a0) for k in range(3)], T.sem.l0)
+    ppf = extract(T.P0, 1, T.G0, 12, True, [g0])
+    pick_add(T.Mb[:, 0:512], T.X[:], nl(0, 512), T.X2[:, 0:512], [ldX, lst, ("x2a", 16)])
+    ma = pick_add(T.Mb[:, 512:1024], T.X[:], nl(512, 1024), T.X2[:, 512:1024], [("x2b", 16)])
+    pf = op("v", [ppf], lambda: V.tensor_scalar(T.PF[:], T.P0[:, 0:12], base, None, A.subtract))
+    mb = pick_add(T.Mb[:, 1024:H], T.X[:], nl(1024, H), T.X2[:, 1024:H], [("x2c", 16)])
+    copy(T.M2[:, 0:1024], T.Mb[:, 0:1024], "m2a", [ma])
+    copy(T.M2[:, 1024:H], T.Mb[:, 1024:H], "m2b", [mb])
+    pick(T.GP[:, 0:1024], T.W[:], tl(0, 1024), [lst])
+    pick(T.G1[:, 0:M3], T.W[:], T.PF[:], [pf])
+    g1 = pick(T.G1[:, M3:2 * M3], T.WZ[:], T.PF[:], [zs])
+    gp = pick(T.GP[:, 1024:H], T.W[:], tl(1024, H), [])
+    ptz = extract(T.P1, 0, T.G1, 24, True, [g1])
+    pl2 = extract(T.P2, 1, T.WZ, 128, True, [zs])
+    ppt = extract(T.P3, 1, T.GP, 128, True, [gp])
+
+    op("v", [ptz], lambda: V.tensor_scalar(T.LS[:, 0:4], T.P1[:, 0:4], base, float(H - 1), A.subtract, A.min))
+    tpf = op("v", [ptz], lambda: V.tensor_scalar(T.LS[:, 16:24], T.P1[:, 4:12], base, float(H - 1), A.subtract, A.min))
+    c1 = op("v", [ptz], lambda: V.tensor_scalar(T.C1[:], T.P1[:, 12:24], 0.0, None, A.is_equal))
+    c2 = op("v", [c1, el], lambda: V.tensor_tensor(T.C2[:], T.C1[:], T.EL[:], A.mult))
+    c3 = op("v", [c2], lambda: V.tensor_tensor(T.C3[:], T.C2[:], T.P1[:, 12:24], A.add))
+    chi = T.ZN[:, blk + O_CODE:blk + O_CODE + 12]
+    clo = T.ZN[:, blk + O_CODE + 12:blk + O_SB]
+    c4 = op("v", [c3], lambda: V.tensor_copy(chi, T.C3[:]))
+    c5 = op("v", [c4], lambda: V.tensor_tensor(clo, T.C3[:], chi, A.subtract))
+    pick(T.ZN[:, blk + O_SB:blk + BLK], T.Mb[:], T.LS[:, 4:24], [ma, mb, tpf])
+    sbe = pick(T.ZN[:, blk:blk + E], T.Mb[:], T.LS[:, 0:4], [])
+    wait("g", [sbe, c5])
+    part = [T.ZN[:, blk + SENT[k][0]:blk + SENT[k][1]] for k in range(3)]
+    send([(pr[k], eng[k], part[k], part[k], T.sem.a1o) for k in range(2)], T.sem.l1)
+    send([(pr[2], eng[2], part[2], part[2], T.sem.a1c)], T.sem.l1)
+
+    uv = op("v", [mb], lambda: V.tensor_copy(T.UE[:, 0:UV], T.Mb[:].indirect(tl(0, UV))))
+    copy(T.U2[:, 0:UV], T.UE[:, 0:UV], "u2", [uv])
+    mid = (UV + H) // 2
+    for a, b in ((UV, mid), (mid, H)):
+        us = pick(T.UE[:, a:b], T.Mb[:], tl(a, b), [])
+        copy(T.U2[:, a:b], T.UE[:, a:b], "u2", [us])
+    pick_add(T.Zb[:, 0:1024], T.Mb[:], nl(0, 1024), T.M2[:, 0:1024], [("m2a", 16)])
+    z = pick_add(T.Zb[:, 1024:H], T.Mb[:], nl(1024, H), T.M2[:, 1024:H], [("m2b", 16)])
+    gta = pick(T.GT[:, 0:1024], T.W[:], nl(0, 1024), [])
+    gtb = pick(T.GT[:, 1024:H], T.W[:], nl(1024, H), [])
+    op("v", [ldN], lambda: V.tensor_scalar(T.NX[:, 0::4], T.AN[:], 4.0, None, A.mult))
+    pa = op("v", [ppt], lambda: V.tensor_scalar(T.PTa[:], T.P3[:, 0:128], base, None, A.subtract))
+    nxv = op("v", [ldA], lambda: V.tensor_scalar(T.NX[:, 3::4], T.AT[:, 128:256], 4.0, 1.0, A.mult, A.add))
+    pb = op("v", [pa, pl2], lambda: V.tensor_tensor(T.PTb[:], T.PTa[:], T.P2[:, 0:128], A.max))
+    gfix = op("v", [ppt, gp, ("a0", n_off + n_on)], lambda: V.tensor_copy(T.GP[:].indirect(far), T.PL[:]))
+    pt16 = op("v", [pb], lambda: V.tensor_copy(T.PT16[:], T.PTb[:]))
+    ppa = extract(T.P5, 1, T.GP, 128, False, [gfix])
+    ptn = extract(T.P4, 0, T.GT, 128, False, [gta], [gtb])
+
+    arr = [("a1o", n_off), ("a1o", n_off), ("a1c", n_on)]
+    for k in (2, 0, 1):
+        c = BLK * pr[k] + O_CODE + 4 * kind[k]
+        cl = op("v", [arr[k]], lambda: V.tensor_tensor(T.CL[:, 4 * k:4 * k + 4], T.ZN[:, c:c + 4], T.ZN[:, c + 12:c + 16], A.add))
+    cl16 = op("v", [cl], lambda: V.tensor_copy(T.CL16[:], T.CL[:]))
+    ufix, ufix2 = us, us
+    for k in (2, 0, 1):
+        c = BLK * pr[k] + O_SB + E * kind[k]
+        lk = T.LS[:, 4 + 4 * k:8 + 4 * k]
+        ufix = op("v", [uv, ufix, ("u2", 48)], lambda: V.tensor_copy(T.UE[:, 0:H].indirect(lk), T.ZN[:, c:c + E]))
+        ufix2 = op("v", [ufix2], lambda: V.tensor_copy(T.U2[:].indirect(lk), T.ZN[:, c:c + E]))
+
+    def even(a, b):
+        return pick(T.Y[:, 2 * a:2 * b:2], T.Zb[:], nl(a, b), [z])
+
+    even(0, 256)
+    ee = pick(T.UE[:, H:H + M3], T.ZN[:], T.CL16[:], [cl16, c5, sbe] + arr + gaps)
+    stores = 0
+    for c in range(len(CH) - 1):
+        a, b = CH[c], CH[c + 1]
+        ye = even(max(a, 256), b)
+        if c == 0:
+            op("s", [ppa], lambda: S.activation(T.NX[:, 2::4], T.P5[:, 0:128], CP, bias=2.0, scale=4.0))
+        if c == 1:
+            nxs = op("s", [ptn], lambda: S.activation(T.NX[:, 1::4], T.P4[:, 0:128], CP, bias=3.0, scale=4.0))
+            copy(T.nx[:], T.NX[:], "st", [nxs, nxv])
+            stores += 16
+        yo = pick_add(T.Y[:, 2 * a + 1:2 * b:2], T.UE[:], T.PT16[:, a // 16:b // 16], T.U2[:, a:b], [ufix, ufix2, ee, pt16])
+        copy(T.y[:, 2 * a:2 * b], T.Y[:, 2 * a:2 * b], "st", [ye, yo])
+        stores += 16
+    wait("g", [("l0", n_off + n_on), ("l1", n_off + n_on)] + [(own[q], count[q]) for q in own] + [("st", stores)])

@@ -5,50 +5,49 @@ H = 2048
 NR = 4
 E = 64
 M3 = 192
-BLK = 408
-O_CODE, O_SB, O_EB, O_EC = 64, 88, 280, 344
-O_E = (0, O_EB, O_EC)
-SENT = ((0, O_EB), (O_CODE, O_EC), (O_CODE, BLK))
-UV = 512
+BLK = 384
+ZW = NR * BLK
+MC = (0, 512, 1024, 1536, 2048)
+US = (("s", 0, 512), ("v", 960, 1504), ("s", 512, 960), ("v", 1504, 2048))
 CH = (0, 512, 1024, 1536, 1792, 2048)
+ROWS = ((0, 1), (0, 2), (4, 5), (6, 7))
 
 SCRATCH = {
     "X": ("sbuf", [128, H], "bfloat16"),
     "X2": ("sbuf", [128, H], "bfloat16"),
+    "B": ("sbuf", [128, H + ZW], "bfloat16"),
     "M2": ("sbuf", [128, H], "bfloat16"),
-    "U2": ("sbuf", [128, H], "bfloat16"),
-    "Mb": ("sbuf", [128, H], "bfloat16"),
     "Zb": ("sbuf", [128, H], "bfloat16"),
     "UE": ("sbuf", [128, H + M3], "bfloat16"),
+    "U2": ("sbuf", [128, H], "bfloat16"),
     "Y": ("sbuf", [128, 2 * H], "bfloat16"),
-    "W": ("sbuf", [128, H], "bfloat16"),
+    "W": ("sbuf", [128, H + M3], "bfloat16"),
     "WZ": ("sbuf", [128, H], "bfloat16"),
     "GP": ("sbuf", [128, H], "bfloat16"),
     "GT": ("sbuf", [128, H], "bfloat16"),
-    "ZN": ("sbuf", [128, NR * BLK], "bfloat16"),
     "G0": ("sbuf", [128, M3], "bfloat16"),
-    "G1": ("sbuf", [128, 2 * M3], "bfloat16"),
-    "PL": ("sbuf", [128, M3], "bfloat16"),
+    "G1": ("sbuf", [128, M3], "bfloat16"),
     "ZT": ("sbuf", [128, M3], "bfloat16"),
     "IOT": ("sbuf", [128, M3], "bfloat16"),
-    "SEL": ("sbuf", [128, 288], "bfloat16"),
+    "SEL": ("sbuf", [128, 576], "bfloat16"),
     "ONES": ("sbuf", [128, 8], "bfloat16"),
-    "T8": ("sbuf", [128, 16], "bfloat16"),
+    "T8": ("sbuf", [128, 24], "bfloat16"),
     "AT": ("sbuf", [128, 256], "int32"),
-    "AN": ("sbuf", [128, 128], "int32"),
-    "IN": ("sbuf", [128, 4, 64], "int32"),
+    "AN": ("sbuf", [128, 256], "int32"),
+    "IN": ("sbuf", [128, 2, 64], "int32"),
     "FAR": ("sbuf", [128, 12], "int32"),
     "HI": ("sbuf", [128, 256], "bfloat16"),
     "LO": ("sbuf", [128, 256], "bfloat16"),
-    "F": ("sbuf", [128, 256], "float32"),
-    "FT": ("sbuf", [128, 256], "float32"),
-    "L": ("sbuf", [128, 256], "uint16"),
+    "F": ("sbuf", [128, 4, 2, 16], "float32"),
+    "FT": ("sbuf", [128, 128], "float32"),
+    "LN": ("sbuf", [128, 128], "uint16"),
+    "LW": ("sbuf", [128, 128], "uint16"),
+    "LU": ("sbuf", [128, 128], "uint16"),
+    "LP": ("sbuf", [128, 128], "uint16"),
     "LS": ("sbuf", [128, 24], "uint16"),
     "PF": ("sbuf", [128, 12], "uint16"),
-    "CL16": ("sbuf", [128, 12], "uint16"),
-    "PT16": ("sbuf", [128, 128], "uint16"),
-    "PTa": ("sbuf", [128, 128], "float32"),
-    "PTb": ("sbuf", [128, 128], "float32"),
+    "CS": ("sbuf", [128, 12], "uint16"),
+    "CL": ("sbuf", [128, 12], "uint16"),
     "KI": ("sbuf", [128, 4], "int32"),
     "KF": ("sbuf", [128, 8], "float32"),
     "IC": ("sbuf", [128, 12], "float32"),
@@ -56,7 +55,6 @@ SCRATCH = {
     "C1": ("sbuf", [128, 12], "float32"),
     "C2": ("sbuf", [128, 12], "float32"),
     "C3": ("sbuf", [128, 12], "float32"),
-    "CL": ("sbuf", [128, 12], "float32"),
     "NX": ("sbuf", [128, 512], "float32"),
     "P0": ("psum", [128, 512], "float32"),
     "P1": ("psum", [128, 512], "float32"),
@@ -64,16 +62,26 @@ SCRATCH = {
     "P3": ("psum", [128, 512], "float32"),
     "P4": ("psum", [128, 512], "float32"),
     "P5": ("psum", [128, 512], "float32"),
+    "P6": ("psum", [128, 512], "float32"),
+    "P7": ("psum", [128, 512], "float32"),
 }
-SEMAPHORES = ["sv", "ss", "sp", "sg", "ldA", "ldF", "ldI", "ldX", "ldN", "ldW", "st", "a0", "a1c", "a1o", "l0", "l1",
-              "x2a", "x2b", "x2c", "m2a", "m2b", "u2"]
+SEMAPHORES = (["sv", "ss", "sp", "sg", "ldA", "ldF", "ldI", "ldX", "ldN", "ldW", "ldZ", "st", "a0", "a1", "a2", "l0"]
+              + ["x2%d" % k for k in range(3)] + ["m2%d" % k for k in range(4)] + ["u2%d" % k for k in range(4)])
 
 
-def peers(T, topo, r):
-    c = T.cores[r]
-    near = [q for q in range(NR) if q != r and T.cores[q] in topo.cores_of(c)]
-    away = [q for q in range(NR) if q != r and q not in near]
-    return away + near
+def others(r):
+    return [q for q in range(NR) if q != r]
+
+
+def layout(T, topo, r):
+    near = [k for k, q in enumerate(others(r)) if T.cores[q] in topo.cores_of(T.cores[r])]
+    if near == [0]:
+        return 2 * E, (0, E, 2 * E + M3)
+    return E, (0, E + M3, 2 * E + M3)
+
+
+def sent(lay, k):
+    return min(lay[0], lay[1][k]), max(lay[0] + M3, lay[1][k] + E)
 
 
 def bits(es):
@@ -110,203 +118,217 @@ def rank_program(g, core, T, topo):
         count[q] += 1
         return (own[q], count[q])
 
-    def copy(out, in_, sem, deps):
-        wait("y", deps)
-        g.sync.dma_start(out, in_).then_inc(T.sem[sem], 16)
+    def copy(out, in_, sem, deps, q="y"):
+        wait(q, deps)
+        Q[q].dma_start(out, in_).then_inc(T.sem[sem], 16)
+        return (sem, 16)
 
     V, S, P = g.vector, g.scalar, g.tensor
     base = float(H * r)
-    pr = peers(T, topo, r)
-    kind = [peers(T, topo, q).index(r) for q in pr]
-    slot = [q - (1 if q > r else 0) for q in pr]
-    blk = BLK * r
+    K = base + H
+    pr = others(r)
+    back = [others(q).index(r) for q in pr]
+    lay = [layout(T, topo, q) for q in range(NR)]
+    o_sb, o_e = lay[r]
+    blk = H + BLK * r
+    near = [k for k in range(3) if T.cores[pr[k]] in topo.cores_of(core)]
+    away = [k for k in range(3) if k not in near]
 
-    g.sync.dma_start(T.AT[:, 0:128], T.twn[:]).then_inc(T.sem.ldA, 16)
-    S.dma_start(T.AT[:, 128:256], T.prv[:]).then_inc(T.sem.ldA, 16)
-    g.sync.dma_start(T.FAR[:], T.far[:]).then_inc(T.sem.ldF, 16)
-    S.dma_start(T.IN[:, 0, :], T.nxt[0::2, :]).then_inc(T.sem.ldI, 16)
-    g.sync.dma_start(T.IN[:, 1, :], T.nxt[1::2, :]).then_inc(T.sem.ldI, 16)
-    S.dma_start(T.IN[:, 2, :], T.twn[0::2, :]).then_inc(T.sem.ldI, 16)
-    g.sync.dma_start(T.IN[:, 3, :], T.twn[1::2, :]).then_inc(T.sem.ldI, 16)
-    S.dma_start(T.X[:], T.x[:]).then_inc(T.sem.ldX, 16)
-    g.sync.dma_start(T.X2[:, 0:512], T.x[:, 0:512]).then_inc(T.sem.x2a, 16)
-    ldA, ldF, ldI, ldX, ldN, ldW = ("ldA", 32), ("ldF", 16), ("ldI", 64), ("ldX", 16), ("ldN", 16), ("ldW", 64)
+    copy(T.AT[0:64, :], T.twn[:], "ldA", [])
+    copy(T.AT[64:128, :], T.prv[:], "ldA", [], "s")
+    copy(T.IN[:, 0, :], T.nxt[0::2, :], "ldI", [])
+    copy(T.IN[:, 1, :], T.nxt[1::2, :], "ldI", [], "s")
+    ldF = copy(T.FAR[:], T.far[:], "ldF", [], "s")
+    ldX = copy(T.X[:], T.x[:], "ldX", [])
+    x2 = [copy(T.X2[:, 0:512], T.x[:, 0:512], "x20", [])]
+    ldA, ldI, ldN, ldW, ldZ = ("ldA", 32), ("ldI", 32), ("ldN", 32), ("ldW", 96), ("ldZ", 32)
 
     ki = op("g", [], lambda: g.iota(T.KI[:, 0:1], [[0, 1]], 0, 1))
     wz0 = op("v", [], lambda: V.memset(T.WZ[:, 0:512], 0.0))
-    sel0 = op("v", [], lambda: V.memset(T.SEL[:], 0.0))
     ones = op("v", [], lambda: V.memset(T.ONES[:], 1.0))
-    r3 = op("v", [ki], lambda: V.tensor_scalar(T.KI[:, 1:2], T.KI[:, 0:1], 3, None, A.bitwise_and))
-    r1 = op("v", [ki], lambda: V.tensor_scalar(T.KI[:, 2:3], T.KI[:, 0:1], 1, None, A.bitwise_and))
-    r15 = op("v", [ki], lambda: V.tensor_scalar(T.KI[:, 3:4], T.KI[:, 0:1], 15, None, A.bitwise_and))
-    w0 = op("v", [], lambda: V.memset(T.W[:], 0.0))
-    op("v", [r15], lambda: V.tensor_copy(T.KF[:, 0:2], T.KI[:, 2:4]))
-    op("v", [r3], lambda: V.tensor_scalar(T.KF[:, 2:3], T.KI[:, 1:2], 2.0, float(H), A.is_equal, A.mult))
-    kf = op("v", [r3], lambda: V.tensor_scalar(T.KF[:, 3:4], T.KI[:, 1:2], 0.0, None, A.is_equal))
+    sel0 = op("v", [], lambda: V.memset(T.SEL[:], 0.0))
+    w0 = op("v", [], lambda: V.memset(T.W[:, 0:H], 0.0))
+    op("v", [ki], lambda: V.tensor_scalar(T.KI[:, 1:2], T.KI[:, 0:1], 1, None, A.bitwise_and))
+    r15 = op("v", [ki], lambda: V.tensor_scalar(T.KI[:, 2:3], T.KI[:, 0:1], 15, None, A.bitwise_and))
 
-    iot = op("g", [], lambda: g.iota(T.IOT[:], [[1, M3]], 0, 0, allow_small_or_imprecise_dtypes=True))
-    t8a = op("g", [ones], lambda: g.affine_select(T.T8[:, 0:8], T.ONES[:], [[-16, 8]], A.is_ge, 0.0, 0, 1))
-    t8b = op("g", [ones], lambda: g.affine_select(T.T8[:, 8:16], T.ONES[:], [[-16, 8]], A.is_ge, 0.0, -2, 1))
-    op("g", [t8a, sel0], lambda: g.affine_select(T.SEL[:, 16:144:16], T.T8[:, 0:8], [[16, 8]], A.is_ge, 0.0, 1, -1))
-    sel = op("g", [t8b, sel0], lambda: g.affine_select(T.SEL[:, 160:288:16], T.T8[:, 8:16], [[16, 8]], A.is_ge, 0.0, 3, -1))
+    low = {}
+    for lo_ in (4, 0, 6):
+        c = 8 * len(low)
+        low[lo_] = (c, op("g", [ones], lambda: g.affine_select(T.T8[:, c:c + 8], T.ONES[:], [[-16, 8]], A.is_ge, 0.0, -lo_, 1)))
+    sel = {}
+    for s in (2, 0, 1, 3):
+        c, d = low[ROWS[s][0]]
+        sel[s] = op("g", [d, sel0], lambda: g.affine_select(T.SEL[:, 144 * s + 16:144 * s + 144:16], T.T8[:, c:c + 8], [[16, 8]],
+                                                            A.is_ge, 0.0, ROWS[s][1], -1))
+        if s == 2:
+            iot = op("g", [], lambda: g.iota(T.IOT[:], [[1, M3]], 0, 0, allow_small_or_imprecise_dtypes=True))
     for k in range(3):
-        ic = op("g", [], lambda: g.iota(T.IC[:, 4 * k:4 * k + 4], [[16, 4]], blk + O_E[k], 0,
+        ic = op("g", [], lambda: g.iota(T.IC[:, 4 * k:4 * k + 4], [[16, 4]], int(K) + BLK * r + o_e[k], 0,
                                         allow_small_or_imprecise_dtypes=True))
 
     for k in range(1, 4):
         wz = op("s", [wz0], lambda: S.activation(T.WZ[:, 512 * k:512 * k + 512], T.WZ[:, 0:512], CP))
     gaps = []
     for k in range(3):
-        lo_, hi_ = SENT[kind[k]]
+        lo_, hi_ = sent(lay[pr[k]], back[k])
+        c = H + BLK * pr[k]
         for a, b in ((0, lo_), (hi_, BLK)):
             if b > a:
-                gaps.append(op("s", [wz0], lambda: S.activation(T.ZN[:, BLK * pr[k] + a:BLK * pr[k] + b], T.WZ[:, 0:b - a], CP)))
-    bcol = []
-    for k in range(3):
-        ck = float(BLK * pr[k] + O_SB + E * kind[k] - E * k)
-        bcol.append(op("s", [kf], lambda: S.activation(T.KF[:, 4 + k:5 + k], T.KF[:, 3:4], ID, bias=T.KF[:, 2:3], scale=ck)))
-    for k in range(3):
-        zt = op("s", [bcol[k], iot, kf], lambda: S.activation(T.ZT[:, E * k:E * k + E], T.IOT[:, E * k:E * k + E], ID,
-                                                              bias=T.KF[:, 4 + k:5 + k], scale=T.KF[:, 0:1]))
+                gaps.append(op("s", [wz0], lambda: S.activation(T.B[:, c + a:c + b], T.WZ[:, 0:b - a], CP)))
 
     hi = op("v", [ldA], lambda: V.tensor_copy(T.HI[:], T.AT[:]))
-    for k in range(3):
-        fl = op("v", [ldF], lambda: V.tensor_copy(T.LS[:, 4 + 4 * k:8 + 4 * k], T.FAR[:, 4 * slot[k]:4 * slot[k] + 4]))
+    op("v", [r15], lambda: V.tensor_copy(T.KF[:, 0:2], T.KI[:, 1:3]))
     lo = op("v", [hi], lambda: V.tensor_tensor(T.LO[:], T.AT[:], T.HI[:], A.subtract))
-    copy(T.W[0::16, :], T.HI[:, 0:128], "ldW", [hi, w0])
-    copy(T.W[2::16, :], T.HI[:, 128:256], "ldW", [])
-    copy(T.W[1::16, :], T.LO[:, 0:128], "ldW", [lo])
-    wait("s", [lo, w0])
-    S.dma_start(T.W[3::16, :], T.LO[:, 128:256]).then_inc(T.sem.ldW, 16)
-    copy(T.X2[:, 512:1024], T.x[:, 512:1024], "x2b", [])
-    copy(T.X2[:, 1024:H], T.x[:, 1024:H], "x2c", [])
-    copy(T.AN[:], T.nxt[:], "ldN", [])
-    el = op("s", [ic, kf], lambda: S.activation(T.EL[:], T.IC[:], ID, bias=T.KF[:, 1:2]))
+    op("v", [r15], lambda: V.tensor_scalar(T.KF[:, 2:3], T.KI[:, 2:3], 2.0, None, A.is_equal))
+    kf = op("v", [r15], lambda: V.tensor_scalar(T.KF[:, 3:4], T.KI[:, 2:3], 6.0, None, A.is_lt))
+    copy(T.W[4::16, 0:H], T.HI[64:128, :], "ldW", [hi, w0])
+    copy(T.W[0::16, 0:H], T.HI[0:64, :], "ldW", [])
+    copy(T.W[6::16, 0:H], T.HI[64:128, :], "ldW", [])
+    copy(T.W[5::16, 0:H], T.LO[64:128, :], "ldW", [lo])
+    copy(T.W[1::16, 0:H], T.LO[0:64, :], "ldW", [lo, w0], "s")
+    copy(T.W[7::16, 0:H], T.LO[64:128, :], "ldW", [])
+    copy(T.WZ[0::16, :], T.HI[0:64, :], "ldZ", [wz, wz0] + gaps)
+    copy(T.WZ[1::16, :], T.LO[0:64, :], "ldZ", [])
+    x2.append(copy(T.X2[:, 512:1024], T.x[:, 512:1024], "x21", []))
+    x2.append(copy(T.X2[:, 1024:H], T.x[:, 1024:H], "x22", []))
+    x2.append(x2[2])
+    copy(T.AN[:, 0:128], T.nxt[:], "ldN", [])
+    copy(T.AN[:, 128:256], T.prv[:], "ldN", [])
 
-    for b in range(4):
-        f = op("v", [ldI], lambda: V.tensor_scalar(T.F[:, 64 * b:64 * b + 64], T.IN[:, :, 16 * b:16 * b + 16], base, None, A.subtract))
+    ev = op("s", [kf], lambda: S.activation(T.KF[:, 4:5], T.KF[:, 0:1], CP, bias=K, scale=-K))
+    bcol = []
+    for k in range(3):
+        dk = float(BLK * pr[k] + lay[pr[k]][0] + E * back[k] - E * k)
+        bcol.append(op("s", [ev], lambda: S.activation(T.KF[:, 5 + k:6 + k], T.KF[:, 2:3], ID, bias=T.KF[:, 4:5], scale=dk - K)))
+    for k in range(3):
+        zt = op("s", [bcol[k], iot], lambda: S.activation(T.ZT[:, E * k:E * k + E], T.IOT[:, E * k:E * k + E], ID,
+                                                          bias=T.KF[:, 5 + k:6 + k], scale=T.KF[:, 0:1]))
+
+    for c in range(2):
+        f = op("v", [ldI], lambda: V.tensor_scalar(T.F[:, :, c, :], T.IN[:, c, :], base, None, A.subtract))
+    far = T.LS[:, o_sb // 16:o_sb // 16 + 12]
+    fl = op("v", [ldF], lambda: V.tensor_copy(far, T.FAR[:]))
     ft = op("v", [f], lambda: V.transpose(T.FT[:], T.F[:]))
     for b in range(4):
-        lst = op("v", [ft], lambda: V.tensor_scalar(T.L[:, b::4], T.FT[:, 64 * b:64 * b + 64], float(H - 1), None, A.min))
-    far = T.LS[:, 4:16]
-    zs = op("v", [fl, zt, wz, wz0] + gaps, lambda: V.tensor_copy(T.WZ[:].indirect(far), T.ZT[:]))
+        lst = op("v", [ft], lambda: V.tensor_copy(T.LN[:, b::4], T.FT[:, 32 * b:32 * b + 32]))
 
-    def nl(a, b):
-        return T.L[:, a // 16:b // 16]
+    def cols(L, a, b):
+        return L[:, a // 16:b // 16]
 
-    def tl(a, b):
-        return T.L[:, 128 + a // 16:128 + b // 16]
-
-    def extract(out, s, src, n, stepped, deps, half=()):
-        wait("p", deps + [sel])
+    def extract(out, s, src, n, step, deps, start=True, stop=True):
+        wait("p", deps + [sel[s]])
         for a in range(16):
-            if a == 8:
-                wait("p", half)
-            rhs = src[:, a:16 * n:16] if stepped else src[:, n * a:n * a + n]
-            ins = P.matmul(out[:, 0:n], T.SEL[:, 144 * s + 16 - a:144 * s + 144 - a], rhs, a == 0, a == 15)
+            rhs = src[:, step + a:step + 16 * n:16] if step is not None else src[:, n * a:n * a + n]
+            ins = P.matmul(out, T.SEL[:, 144 * s + 16 - a:144 * s + 144 - a], rhs, start and a == 0, stop and a == 15)
         ins.then_inc(T.sem.sp, 1)
         count["p"] += 1
         return ("sp", count["p"])
 
-    def pick(out, win, off, deps):
+    def pick(q, out, win, off, deps):
+        if q == "v":
+            return op("v", deps, lambda: V.tensor_copy(out, win.indirect(off)))
         return op("s", deps, lambda: S.activation(out, win.indirect(off), CP))
 
     def pick_add(out, win, off, in1, deps):
         return op("v", deps, lambda: V.tensor_tensor(out, win.indirect(off), in1, A.add))
 
-    def send(parts, lsem):
+    def to_list(out, in_, sub, deps):
+        return op("v", deps, lambda: V.tensor_scalar(out, in_, sub, None, A.subtract))
+
+    off = topo.engines(core, T.cores[pr[away[0]]])
+    on = [e for e in topo.engines(core, T.cores[pr[near[0]]]) if e not in off]
+    eng = {away[0]: off[:len(off) // 2], away[1]: off[len(off) // 2:], near[0]: on}
+    n_all = len(off) + len(on)
+
+    def send(ks, src, dst, sem):
         tr = []
-        for q, es, src, dst, sem in parts:
-            rid, pid = topo.addr(T.cores[q], core)
-            tr.append(RemoteDMATransfer(dst_ids=[DstId(rid=rid, pnc=pid)], dma_engine_mask=bits(es), remote_sem=sem, src=src, dst=dst))
-        g.remote_dma_fused(tr, local_sem=lsem)
+        for k in ks:
+            rid, pid = topo.addr(T.cores[pr[k]], core)
+            tr.append(RemoteDMATransfer(dst_ids=[DstId(rid=rid, pnc=pid)], dma_engine_mask=bits(eng[k]), remote_sem=sem,
+                                        src=src(k), dst=dst(k)))
+        g.remote_dma_fused(tr, local_sem=T.sem.l0)
 
-    off = topo.engines(core, T.cores[pr[0]])
-    on = [e for e in topo.engines(core, T.cores[pr[2]]) if e not in off]
-    eng = [off[:len(off) // 2], off[len(off) // 2:], on]
-    n_off, n_on = len(off), len(on)
+    WL, ML = T.W[:, 0:H], T.B[:, 0:H]
 
-    g0 = pick(T.G0[:], T.W[:], far, [ldW, fl])
+    def m_piece(c, deps=()):
+        a, b = MC[c], MC[c + 1]
+        d = pick_add(T.B[:, a:b], T.X[:], cols(T.LN, a, b), T.X2[:, a:b], [ldX, lst, x2[c]] + list(deps))
+        return d, copy(T.M2[:, a:b], T.B[:, a:b], "m2%d" % c, [d])
+
+    g0 = op("s", [ldW, fl, kf], lambda: S.activation(T.G0[:], WL.indirect(far), ID, scale=T.KF[:, 3:4]))
     wait("g", [g0])
-    send([(pr[k], eng[k], T.G0[:, E * k:E * k + E], T.PL[:, E * kind[k]:E * kind[k] + E], T.sem.a0) for k in range(3)], T.sem.l0)
-    ppf = extract(T.P0, 1, T.G0, 12, True, [g0])
-    pick_add(T.Mb[:, 0:512], T.X[:], nl(0, 512), T.X2[:, 0:512], [ldX, lst, ("x2a", 16)])
-    ma = pick_add(T.Mb[:, 512:1024], T.X[:], nl(512, 1024), T.X2[:, 512:1024], [("x2b", 16)])
-    pf = op("v", [ppf], lambda: V.tensor_scalar(T.PF[:], T.P0[:, 0:12], base, None, A.subtract))
-    mb = pick_add(T.Mb[:, 1024:H], T.X[:], nl(1024, H), T.X2[:, 1024:H], [("x2c", 16)])
-    copy(T.M2[:, 0:1024], T.Mb[:, 0:1024], "m2a", [ma])
-    copy(T.M2[:, 1024:H], T.Mb[:, 1024:H], "m2b", [mb])
-    pick(T.GP[:, 0:1024], T.W[:], tl(0, 1024), [lst])
-    pick(T.G1[:, 0:M3], T.W[:], T.PF[:], [pf])
-    g1 = pick(T.G1[:, M3:2 * M3], T.WZ[:], T.PF[:], [zs])
-    gp = pick(T.GP[:, 1024:H], T.W[:], tl(1024, H), [])
-    ptz = extract(T.P1, 0, T.G1, 24, True, [g1])
-    pl2 = extract(T.P2, 1, T.WZ, 128, True, [zs])
-    ppt = extract(T.P3, 1, T.GP, 128, True, [gp])
+    send(range(3), lambda k: T.G0[:, E * k:E * k + E], lambda k: T.W[:, H + E * back[k]:H + E * back[k] + E], T.sem.a0)
+    ppf = extract(T.P0[:, 0:12], 2, T.G0, 12, 0, [g0])
+    el = op("s", [ic, kf], lambda: S.activation(T.EL[:], T.IC[:], ID, bias=T.KF[:, 1:2]))
+    gta = pick("s", T.GT[:, 0:1024], WL, cols(T.LN, 0, 1024), [lst])
+    m0, m20 = m_piece(0)
+    zs = op("v", [fl, zt, ldZ], lambda: V.tensor_copy(T.WZ[:].indirect(far), T.ZT[:]))
+    pf = to_list(T.PF[:], T.P0[:, 0:12], base, [ppf])
+    m1, m21 = m_piece(1)
+    g1 = pick("s", T.G1[:], T.WZ[:], T.PF[:], [pf, zs])
+    gtb = pick("s", T.GT[:, 1024:H], WL, cols(T.LN, 1024, H), [])
+    pwa = extract(T.P2[:, 0:64], 0, T.WZ, 64, 0, [zs])
+    pg1 = extract(T.P1[:, 0:12], 1, T.G1, 12, 0, [g1])
+    pwb = extract(T.P0[:, 64:128], 0, T.WZ, 64, 1024, [pf])
+    pu = extract(T.P3[:, 0:128], 1, T.WZ, 128, 0, [])
+    extract(T.P4[:, 0:64], 2, T.WZ, 64, 0, [], stop=False)
+    extract(T.P5[:, 0:64], 2, T.WZ, 64, 1024, [], stop=False)
+    ptn = extract(T.P6[:, 0:128], 0, T.GT, 128, None, [gta, gtb])
+    m2, m22 = m_piece(2)
+    lwa = to_list(T.LW[:, 0:64], T.P2[:, 0:64], base, [pwa])
+    nb = o_sb // 16
+    op("v", [pg1], lambda: V.tensor_scalar(T.LS[:, 0:nb], T.P1[:, 0:nb], base, float(H - 1), A.subtract, A.min))
+    tpf = op("v", [pg1], lambda: V.tensor_scalar(T.LS[:, nb + 12:24], T.P1[:, nb:12], base, float(H - 1), A.subtract, A.min))
+    c1 = op("v", [pg1], lambda: V.tensor_scalar(T.C1[:], T.P1[:, 0:12], K, 16384.0, A.is_lt, A.mult))
+    m3, m23 = m_piece(3)
 
-    op("v", [ptz], lambda: V.tensor_scalar(T.LS[:, 0:4], T.P1[:, 0:4], base, float(H - 1), A.subtract, A.min))
-    tpf = op("v", [ptz], lambda: V.tensor_scalar(T.LS[:, 16:24], T.P1[:, 4:12], base, float(H - 1), A.subtract, A.min))
-    c1 = op("v", [ptz], lambda: V.tensor_scalar(T.C1[:], T.P1[:, 12:24], 0.0, None, A.is_equal))
-    c2 = op("v", [c1, el], lambda: V.tensor_tensor(T.C2[:], T.C1[:], T.EL[:], A.mult))
-    c3 = op("v", [c2], lambda: V.tensor_tensor(T.C3[:], T.C2[:], T.P1[:, 12:24], A.add))
-    chi = T.ZN[:, blk + O_CODE:blk + O_CODE + 12]
-    clo = T.ZN[:, blk + O_CODE + 12:blk + O_SB]
-    c4 = op("v", [c3], lambda: V.tensor_copy(chi, T.C3[:]))
-    c5 = op("v", [c4], lambda: V.tensor_tensor(clo, T.C3[:], chi, A.subtract))
-    pick(T.ZN[:, blk + O_SB:blk + BLK], T.Mb[:], T.LS[:, 4:24], [ma, mb, tpf])
-    sbe = pick(T.ZN[:, blk:blk + E], T.Mb[:], T.LS[:, 0:4], [])
-    wait("g", [sbe, c5])
-    part = [T.ZN[:, blk + SENT[k][0]:blk + SENT[k][1]] for k in range(3)]
-    send([(pr[k], eng[k], part[k], part[k], T.sem.a1o) for k in range(2)], T.sem.l1)
-    send([(pr[2], eng[2], part[2], part[2], T.sem.a1c)], T.sem.l1)
+    bv = pick("v", T.B[:, blk:blk + M3], ML, T.LS[:, 0:12], [m3, tpf])
+    bs = pick("s", T.B[:, blk + M3:blk + BLK], ML, T.LS[:, 12:24], [m3, tpf])
+    wait("g", [bv, bs])
 
-    uv = op("v", [mb], lambda: V.tensor_copy(T.UE[:, 0:UV], T.Mb[:].indirect(tl(0, UV))))
-    copy(T.U2[:, 0:UV], T.UE[:, 0:UV], "u2", [uv])
-    mid = (UV + H) // 2
-    for a, b in ((UV, mid), (mid, H)):
-        us = pick(T.UE[:, a:b], T.Mb[:], tl(a, b), [])
-        copy(T.U2[:, a:b], T.UE[:, a:b], "u2", [us])
-    pick_add(T.Zb[:, 0:1024], T.Mb[:], nl(0, 1024), T.M2[:, 0:1024], [("m2a", 16)])
-    z = pick_add(T.Zb[:, 1024:H], T.Mb[:], nl(1024, H), T.M2[:, 1024:H], [("m2b", 16)])
-    gta = pick(T.GT[:, 0:1024], T.W[:], nl(0, 1024), [])
-    gtb = pick(T.GT[:, 1024:H], T.W[:], nl(1024, H), [])
-    op("v", [ldN], lambda: V.tensor_scalar(T.NX[:, 0::4], T.AN[:], 4.0, None, A.mult))
-    pa = op("v", [ppt], lambda: V.tensor_scalar(T.PTa[:], T.P3[:, 0:128], base, None, A.subtract))
-    nxv = op("v", [ldA], lambda: V.tensor_scalar(T.NX[:, 3::4], T.AT[:, 128:256], 4.0, 1.0, A.mult, A.add))
-    pb = op("v", [pa, pl2], lambda: V.tensor_tensor(T.PTb[:], T.PTa[:], T.P2[:, 0:128], A.max))
-    gfix = op("v", [ppt, gp, ("a0", n_off + n_on)], lambda: V.tensor_copy(T.GP[:].indirect(far), T.PL[:]))
-    pt16 = op("v", [pb], lambda: V.tensor_copy(T.PT16[:], T.PTb[:]))
-    ppa = extract(T.P5, 1, T.GP, 128, False, [gfix])
-    ptn = extract(T.P4, 0, T.GT, 128, False, [gta], [gtb])
+    def part(k):
+        a, b = sent(lay[r], k)
+        return T.B[:, blk + a:blk + b]
 
-    arr = [("a1o", n_off), ("a1o", n_off), ("a1c", n_on)]
-    for k in (2, 0, 1):
-        c = BLK * pr[k] + O_CODE + 4 * kind[k]
-        cl = op("v", [arr[k]], lambda: V.tensor_tensor(T.CL[:, 4 * k:4 * k + 4], T.ZN[:, c:c + 4], T.ZN[:, c + 12:c + 16], A.add))
-    cl16 = op("v", [cl], lambda: V.tensor_copy(T.CL16[:], T.CL[:]))
-    ufix, ufix2 = us, us
-    for k in (2, 0, 1):
-        c = BLK * pr[k] + O_SB + E * kind[k]
-        lk = T.LS[:, 4 + 4 * k:8 + 4 * k]
-        ufix = op("v", [uv, ufix, ("u2", 48)], lambda: V.tensor_copy(T.UE[:, 0:H].indirect(lk), T.ZN[:, c:c + E]))
-        ufix2 = op("v", [ufix2], lambda: V.tensor_copy(T.U2[:].indirect(lk), T.ZN[:, c:c + E]))
+    send(away, part, part, T.sem.a1)
+    send(near, part, part, T.sem.a1)
+    c2 = op("v", [c1, el], lambda: V.tensor_tensor(T.C2[:], T.C1[:], T.EL[:], A.min))
+    lwb = to_list(T.LW[:, 64:128], T.P0[:, 64:128], base, [pwb])
+    c3 = op("v", [c2], lambda: V.tensor_tensor(T.C3[:], T.C2[:], T.P1[:, 0:12], A.max))
+    lu = to_list(T.LU[:], T.P3[:, 0:128], base, [pu])
+    cs = to_list(T.CS[:], T.C3[:], K, [c3])
+    wait("g", [cs])
+    send(range(3), lambda k: T.CS[:, 4 * k:4 * k + 4], lambda k: T.CL[:, 4 * back[k]:4 * back[k] + 4], T.sem.a2)
 
-    def even(a, b):
-        return pick(T.Y[:, 2 * a:2 * b:2], T.Zb[:], nl(a, b), [z])
+    gpb = pick("s", T.GP[:, 0:1024], T.W[:], cols(T.LW, 0, 1024), [lwa, ("a0", n_all)])
+    gpc = pick("s", T.GP[:, 1024:H], T.W[:], cols(T.LW, 1024, H), [lwb])
+    ppa = extract(T.P4[:, 0:64], 3, T.GP, 64, 0, [gpb], start=False)
+    ppb = extract(T.P5[:, 0:64], 3, T.GP, 64, 1024, [gpc], start=False)
+    ppt = extract(T.P7[:, 0:128], 2, T.GP, 128, None, [])
+    pick_add(T.Zb[:, 0:1024], ML, cols(T.LN, 0, 1024), T.M2[:, 0:1024], [m20, m21])
+    op("v", [ldN], lambda: V.tensor_scalar(T.NX[:, 0::4], T.AN[:, 0:128], 4.0, None, A.mult))
+    nxv = op("v", [ldN], lambda: V.tensor_scalar(T.NX[:, 3::4], T.AN[:, 128:256], 4.0, 1.0, A.mult, A.add))
+    z = pick_add(T.Zb[:, 1024:H], ML, cols(T.LN, 1024, H), T.M2[:, 1024:H], [m22, m23])
+    lpa = to_list(T.LP[:, 0:64], T.P4[:, 0:64], base, [ppa])
+    op("s", [ptn], lambda: S.activation(T.NX[:, 1::4], T.P6[:, 0:128], CP, bias=3.0, scale=4.0))
 
-    even(0, 256)
-    ee = pick(T.UE[:, H:H + M3], T.ZN[:], T.CL16[:], [cl16, c5, sbe] + arr + gaps)
-    stores = 0
+    here = [("a1", n_all), lu, bv, bs] + gaps
+    u2, last = [], {}
+    for c, (q, a, b) in enumerate(US):
+        last[q] = pick(q, T.UE[:, a:b], T.B[:], cols(T.LU, a, b), here)
+        u2.append((a, b, copy(T.U2[:, a:b], T.UE[:, a:b], "u2%d" % c, [last[q]])))
+    lpb = to_list(T.LP[:, 64:128], T.P5[:, 0:64], base, [ppb])
+    ee = pick("s", T.UE[:, H:H + M3], T.B[:, H:H + ZW], T.CL[:], [("a2", n_all)])
+    nxs = op("s", [ppt], lambda: S.activation(T.NX[:, 2::4], T.P7[:, 0:128], CP, bias=2.0, scale=4.0))
+    copy(T.nx[:], T.NX[:], "st", [nxs, nxv])
+    stores = 16
+
     for c in range(len(CH) - 1):
         a, b = CH[c], CH[c + 1]
-        ye = even(max(a, 256), b)
-        if c == 0:
-            op("s", [ppa], lambda: S.activation(T.NX[:, 2::4], T.P5[:, 0:128], CP, bias=2.0, scale=4.0))
-        if c == 1:
-            nxs = op("s", [ptn], lambda: S.activation(T.NX[:, 1::4], T.P4[:, 0:128], CP, bias=3.0, scale=4.0))
-            copy(T.nx[:], T.NX[:], "st", [nxs, nxv])
-            stores += 16
-        yo = pick_add(T.Y[:, 2 * a + 1:2 * b:2], T.UE[:], T.PT16[:, a // 16:b // 16], T.U2[:, a:b], [ufix, ufix2, ee, pt16])
+        ye = pick("s", T.Y[:, 2 * a:2 * b:2], T.Zb[:], cols(T.LN, a, b), [z])
+        need = [d for a2, b2, d in u2 if a2 < b and b2 > a]
+        yo = pick_add(T.Y[:, 2 * a + 1:2 * b:2], T.UE[:], cols(T.LP, a, b), T.U2[:, a:b],
+                      [last["s"], last["v"], ee, lpa, lpb] + need)
         copy(T.y[:, 2 * a:2 * b], T.Y[:, 2 * a:2 * b], "st", [ye, yo])
         stores += 16
-    wait("g", [("l0", n_off + n_on), ("l1", n_off + n_on)] + [(own[q], count[q]) for q in own] + [("st", stores)])
+    wait("g", [("l0", 3 * n_all)] + [(own[q], count[q]) for q in own] + [("st", stores)])

from concourse.bass import DstId, RemoteDMATransfer
from concourse.mybir import AluOpType, ActivationFunctionType

H = 2048
NR = 4
E = 64
M3 = 192
BLK = 384
ZW = NR * BLK
MC = (0, 512, 1024, 1536, 2048)
US = (("s", 0, 512), ("v", 960, 1504), ("s", 512, 960), ("v", 1504, 2048))
CH = (0, 512, 1024, 1536, 1792, 2048)
ROWS = ((0, 1), (0, 2), (4, 5), (6, 7))

SCRATCH = {
    "X": ("sbuf", [128, H], "bfloat16"),
    "X2": ("sbuf", [128, H], "bfloat16"),
    "B": ("sbuf", [128, H + ZW], "bfloat16"),
    "M2": ("sbuf", [128, H], "bfloat16"),
    "Zb": ("sbuf", [128, H], "bfloat16"),
    "UE": ("sbuf", [128, H + M3], "bfloat16"),
    "U2": ("sbuf", [128, H], "bfloat16"),
    "Y": ("sbuf", [128, 2 * H], "bfloat16"),
    "W": ("sbuf", [128, H + M3], "bfloat16"),
    "WZ": ("sbuf", [128, H], "bfloat16"),
    "GP": ("sbuf", [128, H], "bfloat16"),
    "GT": ("sbuf", [128, H], "bfloat16"),
    "G0": ("sbuf", [128, M3], "bfloat16"),
    "G1": ("sbuf", [128, M3], "bfloat16"),
    "ZT": ("sbuf", [128, M3], "bfloat16"),
    "IOT": ("sbuf", [128, M3], "bfloat16"),
    "SEL": ("sbuf", [128, 576], "bfloat16"),
    "ONES": ("sbuf", [128, 8], "bfloat16"),
    "T8": ("sbuf", [128, 24], "bfloat16"),
    "AT": ("sbuf", [128, 256], "int32"),
    "AN": ("sbuf", [128, 256], "int32"),
    "IN": ("sbuf", [128, 2, 64], "int32"),
    "FAR": ("sbuf", [128, 12], "int32"),
    "HI": ("sbuf", [128, 256], "bfloat16"),
    "LO": ("sbuf", [128, 256], "bfloat16"),
    "F": ("sbuf", [128, 4, 2, 16], "float32"),
    "FT": ("sbuf", [128, 128], "float32"),
    "LN": ("sbuf", [128, 128], "uint16"),
    "LW": ("sbuf", [128, 128], "uint16"),
    "LU": ("sbuf", [128, 128], "uint16"),
    "LP": ("sbuf", [128, 128], "uint16"),
    "LS": ("sbuf", [128, 24], "uint16"),
    "PF": ("sbuf", [128, 12], "uint16"),
    "CS": ("sbuf", [128, 12], "uint16"),
    "CL": ("sbuf", [128, 12], "uint16"),
    "KI": ("sbuf", [128, 4], "int32"),
    "KF": ("sbuf", [128, 8], "float32"),
    "IC": ("sbuf", [128, 12], "float32"),
    "EL": ("sbuf", [128, 12], "float32"),
    "C1": ("sbuf", [128, 12], "float32"),
    "C2": ("sbuf", [128, 12], "float32"),
    "C3": ("sbuf", [128, 12], "float32"),
    "NX": ("sbuf", [128, 512], "float32"),
    "P0": ("psum", [128, 512], "float32"),
    "P1": ("psum", [128, 512], "float32"),
    "P2": ("psum", [128, 512], "float32"),
    "P3": ("psum", [128, 512], "float32"),
    "P4": ("psum", [128, 512], "float32"),
    "P5": ("psum", [128, 512], "float32"),
    "P6": ("psum", [128, 512], "float32"),
    "P7": ("psum", [128, 512], "float32"),
}
SEMAPHORES = (["sv", "ss", "sp", "sg", "ldA", "ldF", "ldI", "ldX", "ldN", "ldW", "ldZ", "st", "a0", "a1", "a2", "l0"]
              + ["x2%d" % k for k in range(3)] + ["m2%d" % k for k in range(4)] + ["u2%d" % k for k in range(4)])


def others(r):
    return [q for q in range(NR) if q != r]


def layout(T, topo, r):
    near = [k for k, q in enumerate(others(r)) if T.cores[q] in topo.cores_of(T.cores[r])]
    if near == [0]:
        return 2 * E, (0, E, 2 * E + M3)
    return E, (0, E + M3, 2 * E + M3)


def sent(lay, k):
    return min(lay[0], lay[1][k]), max(lay[0] + M3, lay[1][k] + E)


def bits(es):
    m = 0
    for e in es:
        m |= 1 << e
    return m


def rank_program(g, core, T, topo):
    r = T.rank_of(core)
    if r is None:
        return
    A = AluOpType
    ID = ActivationFunctionType.Identity
    CP = ActivationFunctionType.Copy
    Q = {"v": g.vector, "s": g.scalar, "p": g.tensor, "g": g, "y": g.sync}
    own = {"v": "sv", "s": "ss", "p": "sp", "g": "sg"}
    count = {"v": 0, "s": 0, "p": 0, "g": 0}
    seen = {k: {} for k in Q}

    def wait(q, deps):
        need = {}
        for s, n in deps:
            need[s] = max(need.get(s, 0), n)
        for s, n in need.items():
            if seen[q].get(s, 0) < n:
                Q[q].wait_ge(T.sem[s], n)
                seen[q][s] = n

    def op(q, deps, make):
        wait(q, deps)
        make().then_inc(T.sem[own[q]], 1)
        count[q] += 1
        return (own[q], count[q])

    def copy(out, in_, sem, deps, q="y"):
        wait(q, deps)
        Q[q].dma_start(out, in_).then_inc(T.sem[sem], 16)
        return (sem, 16)

    V, S, P = g.vector, g.scalar, g.tensor
    base = float(H * r)
    K = base + H
    pr = others(r)
    back = [others(q).index(r) for q in pr]
    lay = [layout(T, topo, q) for q in range(NR)]
    o_sb, o_e = lay[r]
    blk = H + BLK * r
    near = [k for k in range(3) if T.cores[pr[k]] in topo.cores_of(core)]
    away = [k for k in range(3) if k not in near]

    copy(T.AT[0:64, :], T.twn[:], "ldA", [])
    copy(T.AT[64:128, :], T.prv[:], "ldA", [], "s")
    copy(T.IN[:, 0, :], T.nxt[0::2, :], "ldI", [])
    copy(T.IN[:, 1, :], T.nxt[1::2, :], "ldI", [], "s")
    ldF = copy(T.FAR[:], T.far[:], "ldF", [], "s")
    ldX = copy(T.X[:], T.x[:], "ldX", [])
    x2 = [copy(T.X2[:, 0:512], T.x[:, 0:512], "x20", [])]
    ldA, ldI, ldN, ldW, ldZ = ("ldA", 32), ("ldI", 32), ("ldN", 32), ("ldW", 96), ("ldZ", 32)

    ki = op("g", [], lambda: g.iota(T.KI[:, 0:1], [[0, 1]], 0, 1))
    wz0 = op("v", [], lambda: V.memset(T.WZ[:, 0:512], 0.0))
    ones = op("v", [], lambda: V.memset(T.ONES[:], 1.0))
    sel0 = op("v", [], lambda: V.memset(T.SEL[:], 0.0))
    w0 = op("v", [], lambda: V.memset(T.W[:, 0:H], 0.0))
    op("v", [ki], lambda: V.tensor_scalar(T.KI[:, 1:2], T.KI[:, 0:1], 1, None, A.bitwise_and))
    r15 = op("v", [ki], lambda: V.tensor_scalar(T.KI[:, 2:3], T.KI[:, 0:1], 15, None, A.bitwise_and))

    low = {}
    for lo_ in (4, 0, 6):
        c = 8 * len(low)
        low[lo_] = (c, op("g", [ones], lambda: g.affine_select(T.T8[:, c:c + 8], T.ONES[:], [[-16, 8]], A.is_ge, 0.0, -lo_, 1)))
    sel = {}
    for s in (2, 0, 1, 3):
        c, d = low[ROWS[s][0]]
        sel[s] = op("g", [d, sel0], lambda: g.affine_select(T.SEL[:, 144 * s + 16:144 * s + 144:16], T.T8[:, c:c + 8], [[16, 8]],
                                                            A.is_ge, 0.0, ROWS[s][1], -1))
        if s == 2:
            iot = op("g", [], lambda: g.iota(T.IOT[:], [[1, M3]], 0, 0, allow_small_or_imprecise_dtypes=True))
    for k in range(3):
        ic = op("g", [], lambda: g.iota(T.IC[:, 4 * k:4 * k + 4], [[16, 4]], int(K) + BLK * r + o_e[k], 0,
                                        allow_small_or_imprecise_dtypes=True))

    for k in range(1, 4):
        wz = op("s", [wz0], lambda: S.activation(T.WZ[:, 512 * k:512 * k + 512], T.WZ[:, 0:512], CP))
    gaps = []
    for k in range(3):
        lo_, hi_ = sent(lay[pr[k]], back[k])
        c = H + BLK * pr[k]
        for a, b in ((0, lo_), (hi_, BLK)):
            if b > a:
                gaps.append(op("s", [wz0], lambda: S.activation(T.B[:, c + a:c + b], T.WZ[:, 0:b - a], CP)))

    hi = op("v", [ldA], lambda: V.tensor_copy(T.HI[:], T.AT[:]))
    op("v", [r15], lambda: V.tensor_copy(T.KF[:, 0:2], T.KI[:, 1:3]))
    lo = op("v", [hi], lambda: V.tensor_tensor(T.LO[:], T.AT[:], T.HI[:], A.subtract))
    op("v", [r15], lambda: V.tensor_scalar(T.KF[:, 2:3], T.KI[:, 2:3], 2.0, None, A.is_equal))
    kf = op("v", [r15], lambda: V.tensor_scalar(T.KF[:, 3:4], T.KI[:, 2:3], 6.0, None, A.is_lt))
    copy(T.W[4::16, 0:H], T.HI[64:128, :], "ldW", [hi, w0])
    copy(T.W[0::16, 0:H], T.HI[0:64, :], "ldW", [])
    copy(T.W[6::16, 0:H], T.HI[64:128, :], "ldW", [])
    copy(T.W[5::16, 0:H], T.LO[64:128, :], "ldW", [lo])
    copy(T.W[1::16, 0:H], T.LO[0:64, :], "ldW", [lo, w0], "s")
    copy(T.W[7::16, 0:H], T.LO[64:128, :], "ldW", [])
    copy(T.WZ[0::16, :], T.HI[0:64, :], "ldZ", [wz, wz0] + gaps)
    copy(T.WZ[1::16, :], T.LO[0:64, :], "ldZ", [])
    x2.append(copy(T.X2[:, 512:1024], T.x[:, 512:1024], "x21", []))
    x2.append(copy(T.X2[:, 1024:H], T.x[:, 1024:H], "x22", []))
    x2.append(x2[2])
    copy(T.AN[:, 0:128], T.nxt[:], "ldN", [])
    copy(T.AN[:, 128:256], T.prv[:], "ldN", [])

    ev = op("s", [kf], lambda: S.activation(T.KF[:, 4:5], T.KF[:, 0:1], CP, bias=K, scale=-K))
    bcol = []
    for k in range(3):
        dk = float(BLK * pr[k] + lay[pr[k]][0] + E * back[k] - E * k)
        bcol.append(op("s", [ev], lambda: S.activation(T.KF[:, 5 + k:6 + k], T.KF[:, 2:3], ID, bias=T.KF[:, 4:5], scale=dk - K)))
    for k in range(3):
        zt = op("s", [bcol[k], iot], lambda: S.activation(T.ZT[:, E * k:E * k + E], T.IOT[:, E * k:E * k + E], ID,
                                                          bias=T.KF[:, 5 + k:6 + k], scale=T.KF[:, 0:1]))

    for c in range(2):
        f = op("v", [ldI], lambda: V.tensor_scalar(T.F[:, :, c, :], T.IN[:, c, :], base, None, A.subtract))
    far = T.LS[:, o_sb // 16:o_sb // 16 + 12]
    fl = op("v", [ldF], lambda: V.tensor_copy(far, T.FAR[:]))
    ft = op("v", [f], lambda: V.transpose(T.FT[:], T.F[:]))
    for b in range(4):
        lst = op("v", [ft], lambda: V.tensor_copy(T.LN[:, b::4], T.FT[:, 32 * b:32 * b + 32]))

    def cols(L, a, b):
        return L[:, a // 16:b // 16]

    def extract(out, s, src, n, step, deps, start=True, stop=True):
        wait("p", deps + [sel[s]])
        for a in range(16):
            rhs = src[:, step + a:step + 16 * n:16] if step is not None else src[:, n * a:n * a + n]
            ins = P.matmul(out, T.SEL[:, 144 * s + 16 - a:144 * s + 144 - a], rhs, start and a == 0, stop and a == 15)
        ins.then_inc(T.sem.sp, 1)
        count["p"] += 1
        return ("sp", count["p"])

    def pick(q, out, win, off, deps):
        if q == "v":
            return op("v", deps, lambda: V.tensor_copy(out, win.indirect(off)))
        return op("s", deps, lambda: S.activation(out, win.indirect(off), CP))

    def pick_add(out, win, off, in1, deps):
        return op("v", deps, lambda: V.tensor_tensor(out, win.indirect(off), in1, A.add))

    def to_list(out, in_, sub, deps):
        return op("v", deps, lambda: V.tensor_scalar(out, in_, sub, None, A.subtract))

    off = topo.engines(core, T.cores[pr[away[0]]])
    on = [e for e in topo.engines(core, T.cores[pr[near[0]]]) if e not in off]
    eng = {away[0]: off[:len(off) // 2], away[1]: off[len(off) // 2:], near[0]: on}
    n_all = len(off) + len(on)

    def send(ks, src, dst, sem):
        tr = []
        for k in ks:
            rid, pid = topo.addr(T.cores[pr[k]], core)
            tr.append(RemoteDMATransfer(dst_ids=[DstId(rid=rid, pnc=pid)], dma_engine_mask=bits(eng[k]), remote_sem=sem,
                                        src=src(k), dst=dst(k)))
        g.remote_dma_fused(tr, local_sem=T.sem.l0)

    WL, ML = T.W[:, 0:H], T.B[:, 0:H]

    def m_piece(c, deps=()):
        a, b = MC[c], MC[c + 1]
        d = pick_add(T.B[:, a:b], T.X[:], cols(T.LN, a, b), T.X2[:, a:b], [ldX, lst, x2[c]] + list(deps))
        return d, copy(T.M2[:, a:b], T.B[:, a:b], "m2%d" % c, [d])

    g0 = op("s", [ldW, fl, kf], lambda: S.activation(T.G0[:], WL.indirect(far), ID, scale=T.KF[:, 3:4]))
    wait("g", [g0])
    send(range(3), lambda k: T.G0[:, E * k:E * k + E], lambda k: T.W[:, H + E * back[k]:H + E * back[k] + E], T.sem.a0)
    ppf = extract(T.P0[:, 0:12], 2, T.G0, 12, 0, [g0])
    el = op("s", [ic, kf], lambda: S.activation(T.EL[:], T.IC[:], ID, bias=T.KF[:, 1:2]))
    gta = pick("s", T.GT[:, 0:1024], WL, cols(T.LN, 0, 1024), [lst])
    m0, m20 = m_piece(0)
    zs = op("v", [fl, zt, ldZ], lambda: V.tensor_copy(T.WZ[:].indirect(far), T.ZT[:]))
    pf = to_list(T.PF[:], T.P0[:, 0:12], base, [ppf])
    m1, m21 = m_piece(1)
    g1 = pick("s", T.G1[:], T.WZ[:], T.PF[:], [pf, zs])
    gtb = pick("s", T.GT[:, 1024:H], WL, cols(T.LN, 1024, H), [])
    pwa = extract(T.P2[:, 0:64], 0, T.WZ, 64, 0, [zs])
    pg1 = extract(T.P1[:, 0:12], 1, T.G1, 12, 0, [g1])
    pwb = extract(T.P0[:, 64:128], 0, T.WZ, 64, 1024, [pf])
    pu = extract(T.P3[:, 0:128], 1, T.WZ, 128, 0, [])
    extract(T.P4[:, 0:64], 2, T.WZ, 64, 0, [], stop=False)
    extract(T.P5[:, 0:64], 2, T.WZ, 64, 1024, [], stop=False)
    ptn = extract(T.P6[:, 0:128], 0, T.GT, 128, None, [gta, gtb])
    m2, m22 = m_piece(2)
    lwa = to_list(T.LW[:, 0:64], T.P2[:, 0:64], base, [pwa])
    nb = o_sb // 16
    op("v", [pg1], lambda: V.tensor_scalar(T.LS[:, 0:nb], T.P1[:, 0:nb], base, float(H - 1), A.subtract, A.min))
    tpf = op("v", [pg1], lambda: V.tensor_scalar(T.LS[:, nb + 12:24], T.P1[:, nb:12], base, float(H - 1), A.subtract, A.min))
    c1 = op("v", [pg1], lambda: V.tensor_scalar(T.C1[:], T.P1[:, 0:12], K, 16384.0, A.is_lt, A.mult))
    m3, m23 = m_piece(3)

    bv = pick("v", T.B[:, blk:blk + M3], ML, T.LS[:, 0:12], [m3, tpf])
    bs = pick("s", T.B[:, blk + M3:blk + BLK], ML, T.LS[:, 12:24], [m3, tpf])
    wait("g", [bv, bs])

    def part(k):
        a, b = sent(lay[r], k)
        return T.B[:, blk + a:blk + b]

    send(away, part, part, T.sem.a1)
    send(near, part, part, T.sem.a1)
    c2 = op("v", [c1, el], lambda: V.tensor_tensor(T.C2[:], T.C1[:], T.EL[:], A.min))
    lwb = to_list(T.LW[:, 64:128], T.P0[:, 64:128], base, [pwb])
    c3 = op("v", [c2], lambda: V.tensor_tensor(T.C3[:], T.C2[:], T.P1[:, 0:12], A.max))
    lu = to_list(T.LU[:], T.P3[:, 0:128], base, [pu])
    cs = to_list(T.CS[:], T.C3[:], K, [c3])
    wait("g", [cs])
    send(range(3), lambda k: T.CS[:, 4 * k:4 * k + 4], lambda k: T.CL[:, 4 * back[k]:4 * back[k] + 4], T.sem.a2)

    gpb = pick("s", T.GP[:, 0:1024], T.W[:], cols(T.LW, 0, 1024), [lwa, ("a0", n_all)])
    gpc = pick("s", T.GP[:, 1024:H], T.W[:], cols(T.LW, 1024, H), [lwb])
    ppa = extract(T.P4[:, 0:64], 3, T.GP, 64, 0, [gpb], start=False)
    ppb = extract(T.P5[:, 0:64], 3, T.GP, 64, 1024, [gpc], start=False)
    ppt = extract(T.P7[:, 0:128], 2, T.GP, 128, None, [])
    pick_add(T.Zb[:, 0:1024], ML, cols(T.LN, 0, 1024), T.M2[:, 0:1024], [m20, m21])
    op("v", [ldN], lambda: V.tensor_scalar(T.NX[:, 0::4], T.AN[:, 0:128], 4.0, None, A.mult))
    nxv = op("v", [ldN], lambda: V.tensor_scalar(T.NX[:, 3::4], T.AN[:, 128:256], 4.0, 1.0, A.mult, A.add))
    z = pick_add(T.Zb[:, 1024:H], ML, cols(T.LN, 1024, H), T.M2[:, 1024:H], [m22, m23])
    lpa = to_list(T.LP[:, 0:64], T.P4[:, 0:64], base, [ppa])
    op("s", [ptn], lambda: S.activation(T.NX[:, 1::4], T.P6[:, 0:128], CP, bias=3.0, scale=4.0))

    here = [("a1", n_all), lu, bv, bs] + gaps
    u2, last = [], {}
    for c, (q, a, b) in enumerate(US):
        last[q] = pick(q, T.UE[:, a:b], T.B[:], cols(T.LU, a, b), here)
        u2.append((a, b, copy(T.U2[:, a:b], T.UE[:, a:b], "u2%d" % c, [last[q]])))
    lpb = to_list(T.LP[:, 64:128], T.P5[:, 0:64], base, [ppb])
    ee = pick("s", T.UE[:, H:H + M3], T.B[:, H:H + ZW], T.CL[:], [("a2", n_all)])
    nxs = op("s", [ppt], lambda: S.activation(T.NX[:, 2::4], T.P7[:, 0:128], CP, bias=2.0, scale=4.0))
    copy(T.nx[:], T.NX[:], "st", [nxs, nxv])
    stores = 16

    for c in range(len(CH) - 1):
        a, b = CH[c], CH[c + 1]
        ye = pick("s", T.Y[:, 2 * a:2 * b:2], T.Zb[:], cols(T.LN, a, b), [z])
        need = [d for a2, b2, d in u2 if a2 < b and b2 > a]
        yo = pick_add(T.Y[:, 2 * a + 1:2 * b:2], T.UE[:], cols(T.LP, a, b), T.U2[:, a:b],
                      [last["s"], last["v"], ee, lpa, lpb] + need)
        copy(T.y[:, 2 * a:2 * b], T.Y[:, 2 * a:2 * b], "st", [ye, yo])
        stores += 16
    wait("g", [("l0", 3 * n_all)] + [(own[q], count[q]) for q in own] + [("st", stores)])
